import numpy as np
import ml_dtypes


def mxq(x, axis, fmt="e4m3"):
    dtype, down = {"e4m3": (ml_dtypes.float8_e4m3fn, 7), "e5m2": (ml_dtypes.float8_e5m2, 14)}[fmt]
    v = np.moveaxis(np.asarray(x, np.float32).astype(ml_dtypes.bfloat16).astype(np.float64), axis, -1)
    blocks = v.reshape(v.shape[:-1] + (-1, 32))
    amax = np.abs(blocks).max(-1, keepdims=True)
    byte = np.maximum(np.where(amax > 0, np.frexp(amax)[1] - 1 + 127, 0) - down, 1)
    scale = np.exp2(byte - 127.0)
    codes = (blocks / scale).astype(np.float32).astype(dtype).astype(np.float64)
    return np.moveaxis((codes * scale).reshape(v.shape), -1, axis)


WIDE = False


def mx_kscale(k):
    if not WIDE:
        return np.ones(k)
    levels = np.array([10, -10, 5, -5, 0])
    if k % 512:
        return np.exp2(np.random.permutation(np.resize(levels, k // 32))).repeat(32)
    a = np.empty((k // 512, 16))
    for p in range(k // 512):
        a[p, :8] = np.random.permutation(np.resize(levels, 8))
        for g in range(8):
            far = levels[np.abs(levels - a[p, g]) >= 10]
            a[p, g + 8] = far[np.random.randint(len(far))]
    return np.exp2(a.ravel()).repeat(32)


def f64(x):
    return np.asarray(x).astype(np.float64)


def striped(idx):
    return np.tile(idx.reshape(-1, 16).T, (8, 1)).astype(np.uint16)


def unstriped(offs):
    return offs[:16].T.reshape(-1).astype(np.int64)


E2M1 = np.array([0.0, 0.5, 1.0, 1.5, 2.0, 3.0, 4.0, 6.0, -0.0, -0.5, -1.0, -1.5, -2.0, -3.0, -4.0, -6.0])


def pack_weight(w, fmt):
    k, n = w.shape
    w = f64(np.asarray(w, np.float32).astype(ml_dtypes.bfloat16)).reshape(k // 32, 32, n)
    amax = np.abs(w).max(1)
    if fmt == "e4m3":
        byte = np.frexp(amax)[1] - 1 + 127 - 7
    else:
        mant, ex = np.frexp(amax / 6.0)
        byte = np.where(mant > 0.5, ex, ex - 1) + 127
    byte = np.clip(np.where(amax > 0, byte, 1), 1, 254)
    scaled = (w * np.exp2(127.0 - byte)[:, None, :]).reshape(k, n).astype(np.float32)
    by_word = np.ascontiguousarray(scaled.reshape(k // 512, 128, 4, n).transpose(0, 1, 3, 2))
    if fmt == "e4m3":
        words = by_word.astype(ml_dtypes.float8_e4m3fn).view(np.uint8)
    else:
        c = by_word.astype(ml_dtypes.float4_e2m1fn).view(np.uint8) & 0xF
        words = (c[..., 0::2] | (c[..., 1::2] << 4)).reshape(k // 512, 128, 2 * n)
    return np.ascontiguousarray(words), np.ascontiguousarray(byte.astype(np.uint8).reshape(k // 512, 16, n))


def unpack_weight(words, scales, fmt):
    g, _, n = scales.shape
    words = np.ascontiguousarray(words).reshape(g, 128, n, -1)
    if fmt == "e4m3":
        vals = words.view(ml_dtypes.float8_e4m3fn).astype(np.float64)
    else:
        nib = np.empty((g, 128, n, 4), np.uint8)
        nib[..., 0::2] = words & 0xF
        nib[..., 1::2] = words >> 4
        vals = E2M1[nib]
    vals = vals * np.repeat(np.exp2(scales.astype(np.float64) - 127.0), 8, axis=1)[..., None]
    return vals.transpose(0, 1, 3, 2).reshape(g * 512, n)


def gelu(v):
    return 0.5 * v * (1.0 + np.tanh(np.sqrt(2.0 / np.pi) * (v + 0.044715 * v**3)))


K, T, E, C, N = 2048, 768, 2, 256, 128


def by_expert(wq, xq):
    return np.concatenate([wq[e].T @ xq[:, e * C:(e + 1) * C] for e in range(E)], axis=1)


def setup_inputs():
    n = np.random.standard_normal
    s = mx_kscale(K)[:, None]
    x = pack_weight(n((K, T)) * s, "e4m3")
    return {
        "x_words": x[0],
        "x_scales": x[1],
        "w": (n((E, K, N)) / np.sqrt(K) / s[None]).astype(np.float32),
        "b": (0.3 * n((N, E))).astype(np.float32),
        "gate": np.tile(np.random.uniform(0.2, 1.0, E * C), (N, 1)).astype(np.float32),
        "offs": striped(np.random.permutation(T)[:E * C]),
    }


def reference(x_words, x_scales, w, b, gate, offs):
    idx = unstriped(offs)
    xq = unpack_weight(x_words, x_scales, "e4m3")[:, idx]
    y = by_expert(mxq(f64(w), 1, "e4m3"), xq)
    y = gelu(y + np.repeat(f64(b), C, axis=1))
    out = np.zeros((N, T))
    out[:, idx] = f64(gate) * y
    return out

@@ -1,0 +1,178 @@
+from contextlib import ExitStack
+
+import concourse.mybir as mybir
+
+K, T, E, C, N = 2048, 768, 2, 256, 128
+S = E * C
+FLOPS = 2 * K * N * S
+
+F32 = mybir.dt.float32
+BF16 = mybir.dt.bfloat16
+I32 = mybir.dt.int32
+U32 = mybir.dt.uint32
+U16 = mybir.dt.uint16
+U8 = mybir.dt.uint8
+FP8X4 = mybir.dt.float8_e4m3fn_x4
+GELU = mybir.ActivationFunctionType.Gelu_apprx_tanh
+MULT = mybir.AluOpType.mult
+
+P = 128
+PACK = 4
+K_PASS = P * PACK
+PASSES = K // K_PASS
+LIST_ROWS = 16
+
+
+def tile_moe_pkd_lin_gelu_kernel(tc, x_words, x_scales, w, b, gate, offs, out):
+    nc = tc.nc
+    with ExitStack() as ctx:
+        keep = ctx.enter_context(tc.tile_pool(name="keep", bufs=1))
+        psum = ctx.enter_context(tc.psum_pool(name="psum", bufs=1))
+
+        offsets = keep.tile([P, S // LIST_ROWS], U16, name="offsets")
+        nc.sync.dma_start(offsets[:], offs)
+
+        def entries(first, count):
+            return offsets[:, first // LIST_ROWS : (first + count) // LIST_ROWS]
+
+        token_scales = keep.tile([P, T], U8, name="token_scales", align_bytes=64)
+        nc.vector.memset(token_scales[:].bitcast(I32), 0)
+        scale_rows = x_scales.bitcast(I32)
+        for q in range(4):
+            nc.scalar.dma_start(
+                out=token_scales[32 * q : 32 * q + 16, :].bitcast(I32),
+                in_=scale_rows[:, 4 * q : 4 * q + 4, :],
+            )
+
+        zero = keep.tile([P, 1], F32, name="zero")
+        nc.vector.memset(zero[:], 0.0)
+        result = keep.tile([P, T], F32, name="result", align_bytes=64)
+        nc.scalar.activation(out=result[:], in_=zero[:].to_broadcast([P, T]), func=GELU)
+
+        token_words = [keep.tile([P, T], I32, name="token_words%d" % o, align_bytes=64) for o in range(PASSES)]
+        w_raw = {
+            (e, o): keep.tile([P, PACK, N], F32, name="w_raw%d%d" % (e, o), align_bytes=64)
+            for e in range(E)
+            for o in range(PASSES)
+        }
+        w_bf16 = {
+            (e, o): keep.tile([P, N, PACK], BF16, name="w_bf16_%d%d" % (e, o), align_bytes=64)
+            for e in range(E)
+            for o in range(PASSES)
+        }
+        w_codes = {
+            (e, o): keep.tile([P, N], U32, name="w_codes%d%d" % (e, o), align_bytes=64)
+            for e in range(E)
+            for o in range(PASSES)
+        }
+        w_scales = {
+            (e, o): keep.tile([P, N], U8, name="w_scales%d%d" % (e, o), align_bytes=64)
+            for e in range(E)
+            for o in range(PASSES)
+        }
+        slot_words = [keep.tile([P, S], U32, name="slot_words%d" % o, align_bytes=64) for o in range(PASSES)]
+        slot_scales = keep.tile([P, S], U8, name="slot_scales", align_bytes=64)
+        bias = keep.tile([P, E], F32, name="bias")
+        gates = [keep.tile([P, C], F32, name="gates%d" % e, align_bytes=64) for e in range(E)]
+        activated = [keep.tile([P, C], F32, name="activated%d" % e, align_bytes=64) for e in range(E)]
+        sums = [psum.tile([P, C], F32, name="sums%d" % e) for e in range(E)]
+
+        def load_tokens(o):
+            nc.sync.dma_start(out=token_words[o][:], in_=x_words[o].rearrange("p t r -> p (t r)").bitcast(I32))
+
+        def load_weights(e, o):
+            rows = w[e, o * K_PASS : (o + 1) * K_PASS, :]
+            nc.sync.dma_start(out=w_raw[e, o][:], in_=rows.rearrange("(p j) n -> p j n", j=PACK))
+
+        def load_gate(e):
+            nc.sync.dma_start(out=gates[e][:], in_=gate[:, e * C : (e + 1) * C])
+
+        def cast_weights(e, o):
+            nc.scalar.copy(
+                out=w_bf16[e, o][:].rearrange("p (c i) j -> p c j i", i=4),
+                in_=w_raw[e, o][:].rearrange("p j (c i) -> p c j i", i=4),
+            )
+
+        def quantize_weights(e, o):
+            nc.vector.quantize_mx(
+                out=w_codes[e, o][:].bitcast(FP8X4),
+                scales=w_scales[e, o][:],
+                in_=w_bf16[e, o][:].rearrange("p n j -> p (n j)"),
+            )
+
+        def gather_words(o, first, count):
+            nc.vector.tensor_copy(
+                slot_words[o][:, first : first + count],
+                token_words[o][:].bitcast(U32).indirect(entries(first, count)),
+            )
+
+        def multiply(e, o):
+            slots = slice(e * C, (e + 1) * C)
+            nc.tensor.matmul_mx(
+                out=sums[e][:],
+                lhsT=w_codes[e, o][:].bitcast(FP8X4),
+                lhsT_scale=w_scales[e, o][:],
+                rhs=slot_words[o][:, slots].bitcast(FP8X4),
+                rhs_scale=slot_scales[4 * o : P, slots],
+                start=(o == 0),
+                stop=(o == PASSES - 1),
+            )
+
+        def activate(e):
+            nc.scalar.activation(out=activated[e][:], in_=sums[e][:], func=GELU, bias=bias[:, e : e + 1])
+
+        def scatter(e, first, count):
+            nc.vector.tensor_tensor(
+                result[:].indirect(entries(e * C + first, count)),
+                activated[e][:, first : first + count],
+                gates[e][:, first : first + count],
+                MULT,
+            )
+
+        load_tokens(0)
+        load_weights(0, 0)
+        load_tokens(1)
+        load_weights(0, 1)
+        load_weights(0, 2)
+        load_tokens(2)
+        load_weights(0, 3)
+        nc.sync.dma_start(out=bias[:], in_=b)
+        load_weights(1, 0)
+        load_tokens(3)
+        load_gate(0)
+        load_weights(1, 1)
+        load_weights(1, 2)
+        load_weights(1, 3)
+        load_gate(1)
+        nc.vector.tensor_copy(slot_scales[:], token_scales[:].indirect(offsets[:]))
+        gather_words(0, 0, S)
+        gather_words(1, 0, S)
+        cast_weights(0, 0)
+        cast_weights(0, 1)
+        quantize_weights(0, 0)
+        quantize_weights(0, 1)
+        gather_words(2, 0, S)
+        cast_weights(0, 2)
+        cast_weights(0, 3)
+        cast_weights(1, 0)
+        quantize_weights(0, 2)
+        quantize_weights(0, 3)
+        gather_words(3, 0, C)
+        gather_words(3, C, C)
+        for o in range(PASSES):
+            multiply(0, o)
+        cast_weights(1, 1)
+        activate(0)
+        quantize_weights(1, 0)
+        quantize_weights(1, 1)
+        cast_weights(1, 2)
+        cast_weights(1, 3)
+        scatter(0, 0, C // 2)
+        quantize_weights(1, 2)
+        quantize_weights(1, 3)
+        scatter(0, C // 2, C // 2)
+        for o in range(PASSES):
+            multiply(1, o)
+        activate(1)
+        scatter(1, 0, C)
+        nc.sync.dma_start(out=out, in_=result[:])

@@ -1,6 +1,7 @@
 from contextlib import ExitStack
 
 import concourse.mybir as mybir
+from concourse.masks import make_identity
 
 K, T, E, C, N = 2048, 768, 2, 256, 128
 S = E * C
@@ -30,19 +31,20 @@ def tile_moe_pkd_lin_gelu_kernel(tc, x_words, x_scales, w, b, gate, offs, out):
         psum = ctx.enter_context(tc.psum_pool(name="psum", bufs=1))
 
         offsets = keep.tile([P, S // LIST_ROWS], U16, name="offsets")
-        nc.sync.dma_start(offsets[:], offs)
 
         def entries(first, count):
             return offsets[:, first // LIST_ROWS : (first + count) // LIST_ROWS]
 
         token_scales = keep.tile([P, T], U8, name="token_scales", align_bytes=64)
-        nc.vector.memset(token_scales[:].bitcast(I32), 0)
-        scale_rows = x_scales.bitcast(I32)
-        for q in range(4):
-            nc.scalar.dma_start(
-                out=token_scales[32 * q : 32 * q + 16, :].bitcast(I32),
-                in_=scale_rows[:, 4 * q : 4 * q + 4, :],
-            )
+        nc.gpsimd.memset(token_scales[:].bitcast(I32), 0)
+
+        def load_scales():
+            scale_rows = x_scales.bitcast(I32)
+            for q in range(4):
+                nc.sync.dma_start(
+                    out=token_scales[32 * q : 32 * q + 16, :].bitcast(I32),
+                    in_=scale_rows[:, 4 * q : 4 * q + 4, :],
+                )
 
         zero = keep.tile([P, 1], F32, name="zero")
         nc.vector.memset(zero[:], 0.0)
@@ -50,11 +52,7 @@ def tile_moe_pkd_lin_gelu_kernel(tc, x_words, x_scales, w, b, gate, offs, out):
         nc.scalar.activation(out=result[:], in_=zero[:].to_broadcast([P, T]), func=GELU)
 
         token_words = [keep.tile([P, T], I32, name="token_words%d" % o, align_bytes=64) for o in range(PASSES)]
-        w_raw = {
-            (e, o): keep.tile([P, PACK, N], F32, name="w_raw%d%d" % (e, o), align_bytes=64)
-            for e in range(E)
-            for o in range(PASSES)
-        }
+        w_raw = {}
         w_bf16 = {
             (e, o): keep.tile([P, N, PACK], BF16, name="w_bf16_%d%d" % (e, o), align_bytes=64)
             for e in range(E)
@@ -73,24 +71,42 @@ def tile_moe_pkd_lin_gelu_kernel(tc, x_words, x_scales, w, b, gate, offs, out):
         slot_words = [keep.tile([P, S], U32, name="slot_words%d" % o, align_bytes=64) for o in range(PASSES)]
         slot_scales = keep.tile([P, S], U8, name="slot_scales", align_bytes=64)
         bias = keep.tile([P, E], F32, name="bias")
-        gates = [keep.tile([P, C], F32, name="gates%d" % e, align_bytes=64) for e in range(E)]
-        activated = [keep.tile([P, C], F32, name="activated%d" % e, align_bytes=64) for e in range(E)]
-        sums = [psum.tile([P, C], F32, name="sums%d" % e) for e in range(E)]
+        gates = keep.tile([P, S], F32, name="gates", align_bytes=64)
+        gate_columns = keep.tile([P, S // P], F32, name="gate_columns", align_bytes=64)
+        identity = keep.tile([P, P], F32, name="identity", align_bytes=64)
+        make_identity(nc, identity[:])
+        activated = {}
+        sums = {}
 
         def load_tokens(o):
             nc.sync.dma_start(out=token_words[o][:], in_=x_words[o].rearrange("p t r -> p (t r)").bitcast(I32))
 
-        def load_weights(e, o):
-            rows = w[e, o * K_PASS : (o + 1) * K_PASS, :]
-            nc.sync.dma_start(out=w_raw[e, o][:], in_=rows.rearrange("(p j) n -> p j n", j=PACK))
+        def load_weights(e, first, count, tag=""):
+            raw = keep.tile([P, count, PACK, N], F32, name="w_raw%d%d" % (e, first), tag=tag, align_bytes=64)
+            rows = w[e, first * K_PASS : (first + count) * K_PASS, :]
+            nc.sync.dma_start(
+                out=raw[:].rearrange("p o j n -> p o (j n)"),
+                in_=rows.rearrange("(o p j) n -> p o (j n)", p=P, j=PACK),
+            )
+            for o in range(count):
+                w_raw[e, first + o] = raw[:, o]
 
-        def load_gate(e):
-            nc.sync.dma_start(out=gates[e][:], in_=gate[:, e * C : (e + 1) * C])
+        def load_gate():
+            nc.sync.dma_start(out=gate_columns[:], in_=gate[0].rearrange("(p m) -> p m", p=P))
 
-        def cast_weights(e, o):
+        def spread_gate():
+            spread = psum.tile([P, S // P, P], F32, name="spread", tag="bank0")
+            for m in range(S // P):
+                nc.tensor.transpose(spread[:, m, :], gate_columns[:, m : m + 1].to_broadcast([P, P]), identity[:])
             nc.scalar.copy(
+                out=gates[:].rearrange("q (p m) -> q p m", p=P),
+                in_=spread[:].rearrange("q m p -> q p m"),
+            )
+
+        def cast_weights(e, o, copy=nc.scalar.copy):
+            copy(
                 out=w_bf16[e, o][:].rearrange("p (c i) j -> p c j i", i=4),
-                in_=w_raw[e, o][:].rearrange("p j (c i) -> p c j i", i=4),
+                in_=w_raw[e, o].rearrange("p j (c i) -> p c j i", i=4),
             )
 
         def quantize_weights(e, o):
@@ -108,6 +124,8 @@ def tile_moe_pkd_lin_gelu_kernel(tc, x_words, x_scales, w, b, gate, offs, out):
 
         def multiply(e, o):
             slots = slice(e * C, (e + 1) * C)
+            if o == 0:
+                sums[e] = psum.tile([P, C], F32, name="sums%d" % e, tag="bank%d" % e)
             nc.tensor.matmul_mx(
                 out=sums[e][:],
                 lhsT=w_codes[e, o][:].bitcast(FP8X4),
@@ -118,61 +136,66 @@ def tile_moe_pkd_lin_gelu_kernel(tc, x_words, x_scales, w, b, gate, offs, out):
                 stop=(o == PASSES - 1),
             )
 
-        def activate(e):
-            nc.scalar.activation(out=activated[e][:], in_=sums[e][:], func=GELU, bias=bias[:, e : e + 1])
+        def activate(e, first, count, tag=""):
+            values = keep.tile([P, count], F32, name="activated%d_%d" % (e, first), tag=tag, align_bytes=64)
+            nc.scalar.activation(
+                out=values[:], in_=sums[e][:, first : first + count], func=GELU, bias=bias[:, e : e + 1]
+            )
+            activated[e, first] = values
 
         def scatter(e, first, count):
             nc.vector.tensor_tensor(
                 result[:].indirect(entries(e * C + first, count)),
-                activated[e][:, first : first + count],
-                gates[e][:, first : first + count],
+                activated[e, first][:],
+                gates[:, e * C + first : e * C + first + count],
                 MULT,
             )
 
         load_tokens(0)
-        load_weights(0, 0)
+        nc.sync.dma_start(offsets[:], offs)
+        load_scales()
+        load_weights(0, 0, 2)
         load_tokens(1)
-        load_weights(0, 1)
-        load_weights(0, 2)
-        load_tokens(2)
-        load_weights(0, 3)
+        load_weights(0, 2, 2)
+        load_gate()
         nc.sync.dma_start(out=bias[:], in_=b)
-        load_weights(1, 0)
+        load_tokens(2)
         load_tokens(3)
-        load_gate(0)
-        load_weights(1, 1)
-        load_weights(1, 2)
-        load_weights(1, 3)
-        load_gate(1)
-        nc.vector.tensor_copy(slot_scales[:], token_scales[:].indirect(offsets[:]))
+        load_weights(1, 0, 1)
+        load_weights(1, 1, 1, tag="second")
+        load_weights(1, 2, 1)
+        load_weights(1, 3, 1, tag="last")
         gather_words(0, 0, S)
-        gather_words(1, 0, S)
+        nc.vector.tensor_copy(slot_scales[:], token_scales[:].indirect(offsets[:]))
         cast_weights(0, 0)
         cast_weights(0, 1)
         quantize_weights(0, 0)
+        gather_words(1, 0, S)
         quantize_weights(0, 1)
-        gather_words(2, 0, S)
         cast_weights(0, 2)
         cast_weights(0, 3)
-        cast_weights(1, 0)
+        spread_gate()
         quantize_weights(0, 2)
+        gather_words(2, 0, S)
         quantize_weights(0, 3)
         gather_words(3, 0, C)
         gather_words(3, C, C)
         for o in range(PASSES):
             multiply(0, o)
+        cast_weights(1, 0)
         cast_weights(1, 1)
-        activate(0)
         quantize_weights(1, 0)
         quantize_weights(1, 1)
-        cast_weights(1, 2)
-        cast_weights(1, 3)
+        activate(0, 0, C // 2, tag="second")
         scatter(0, 0, C // 2)
+        cast_weights(1, 2)
         quantize_weights(1, 2)
+        cast_weights(1, 3)
         quantize_weights(1, 3)
+        activate(0, C // 2, C // 2, tag="last")
         scatter(0, C // 2, C // 2)
         for o in range(PASSES):
             multiply(1, o)
-        activate(1)
+        activate(1, 0, C)
         scatter(1, 0, C)
         nc.sync.dma_start(out=out, in_=result[:])

@@ -156,13 +156,14 @@ def tile_moe_pkd_lin_gelu_kernel(tc, x_words, x_scales, w, b, gate, offs, out):
         load_scales()
         load_weights(0, 0, 2)
         load_tokens(1)
-        load_weights(0, 2, 2)
         load_gate()
-        nc.sync.dma_start(out=bias[:], in_=b)
+        load_weights(0, 2, 1)
         load_tokens(2)
+        load_weights(0, 3, 1)
         load_tokens(3)
-        load_weights(1, 0, 1)
-        load_weights(1, 1, 1, tag="second")
+        nc.sync.dma_start(out=bias[:], in_=b)
+        load_weights(1, 0, 1, tag="second")
+        load_weights(1, 1, 1)
         load_weights(1, 2, 1)
         load_weights(1, 3, 1, tag="last")
         gather_words(0, 0, S)
@@ -172,9 +173,9 @@ def tile_moe_pkd_lin_gelu_kernel(tc, x_words, x_scales, w, b, gate, offs, out):
         quantize_weights(0, 0)
         gather_words(1, 0, S)
         quantize_weights(0, 1)
+        spread_gate()
         cast_weights(0, 2)
         cast_weights(0, 3)
-        spread_gate()
         quantize_weights(0, 2)
         gather_words(2, 0, S)
         quantize_weights(0, 3)
@@ -183,12 +184,12 @@ def tile_moe_pkd_lin_gelu_kernel(tc, x_words, x_scales, w, b, gate, offs, out):
         for o in range(PASSES):
             multiply(0, o)
         cast_weights(1, 0)
-        cast_weights(1, 1)
         quantize_weights(1, 0)
-        quantize_weights(1, 1)
         activate(0, 0, C // 2, tag="second")
         scatter(0, 0, C // 2)
-        cast_weights(1, 2)
+        cast_weights(1, 1)
+        cast_weights(1, 2, nc.vector.tensor_copy)
+        quantize_weights(1, 1)
         quantize_weights(1, 2)
         cast_weights(1, 3)
         quantize_weights(1, 3)

from contextlib import ExitStack

import concourse.mybir as mybir
from concourse.masks import make_identity

K, T, E, C, N = 2048, 768, 2, 256, 128
S = E * C
FLOPS = 2 * K * N * S

F32 = mybir.dt.float32
BF16 = mybir.dt.bfloat16
I32 = mybir.dt.int32
U32 = mybir.dt.uint32
U16 = mybir.dt.uint16
U8 = mybir.dt.uint8
FP8X4 = mybir.dt.float8_e4m3fn_x4
GELU = mybir.ActivationFunctionType.Gelu_apprx_tanh
MULT = mybir.AluOpType.mult

P = 128
PACK = 4
K_PASS = P * PACK
PASSES = K // K_PASS
LIST_ROWS = 16


def tile_moe_pkd_lin_gelu_kernel(tc, x_words, x_scales, w, b, gate, offs, out):
    nc = tc.nc
    with ExitStack() as ctx:
        keep = ctx.enter_context(tc.tile_pool(name="keep", bufs=1))
        psum = ctx.enter_context(tc.psum_pool(name="psum", bufs=1))

        offsets = keep.tile([P, S // LIST_ROWS], U16, name="offsets")

        def entries(first, count):
            return offsets[:, first // LIST_ROWS : (first + count) // LIST_ROWS]

        token_scales = keep.tile([P, T], U8, name="token_scales", align_bytes=64)
        nc.gpsimd.memset(token_scales[:].bitcast(I32), 0)

        def load_scales():
            scale_rows = x_scales.bitcast(I32)
            for q in range(4):
                nc.sync.dma_start(
                    out=token_scales[32 * q : 32 * q + 16, :].bitcast(I32),
                    in_=scale_rows[:, 4 * q : 4 * q + 4, :],
                )

        zero = keep.tile([P, 1], F32, name="zero")
        nc.vector.memset(zero[:], 0.0)
        result = keep.tile([P, T], F32, name="result", align_bytes=64)
        nc.scalar.activation(out=result[:], in_=zero[:].to_broadcast([P, T]), func=GELU)

        token_words = [keep.tile([P, T], I32, name="token_words%d" % o, align_bytes=64) for o in range(PASSES)]
        w_raw = {}
        w_bf16 = {
            (e, o): keep.tile([P, N, PACK], BF16, name="w_bf16_%d%d" % (e, o), align_bytes=64)
            for e in range(E)
            for o in range(PASSES)
        }
        w_codes = {
            (e, o): keep.tile([P, N], U32, name="w_codes%d%d" % (e, o), align_bytes=64)
            for e in range(E)
            for o in range(PASSES)
        }
        w_scales = {
            (e, o): keep.tile([P, N], U8, name="w_scales%d%d" % (e, o), align_bytes=64)
            for e in range(E)
            for o in range(PASSES)
        }
        slot_words = [keep.tile([P, S], U32, name="slot_words%d" % o, align_bytes=64) for o in range(PASSES)]
        slot_scales = keep.tile([P, S], U8, name="slot_scales", align_bytes=64)
        bias = keep.tile([P, E], F32, name="bias")
        gates = keep.tile([P, S], F32, name="gates", align_bytes=64)
        gate_columns = keep.tile([P, S // P], F32, name="gate_columns", align_bytes=64)
        identity = keep.tile([P, P], F32, name="identity", align_bytes=64)
        make_identity(nc, identity[:])
        activated = {}
        sums = {}

        def load_tokens(o):
            nc.sync.dma_start(out=token_words[o][:], in_=x_words[o].rearrange("p t r -> p (t r)").bitcast(I32))

        def load_weights(e, first, count, tag=""):
            raw = keep.tile([P, count, PACK, N], F32, name="w_raw%d%d" % (e, first), tag=tag, align_bytes=64)
            rows = w[e, first * K_PASS : (first + count) * K_PASS, :]
            nc.sync.dma_start(
                out=raw[:].rearrange("p o j n -> p o (j n)"),
                in_=rows.rearrange("(o p j) n -> p o (j n)", p=P, j=PACK),
            )
            for o in range(count):
                w_raw[e, first + o] = raw[:, o]

        def load_gate():
            nc.sync.dma_start(out=gate_columns[:], in_=gate[0].rearrange("(p m) -> p m", p=P))

        def spread_gate():
            spread = psum.tile([P, S // P, P], F32, name="spread", tag="bank0")
            for m in range(S // P):
                nc.tensor.transpose(spread[:, m, :], gate_columns[:, m : m + 1].to_broadcast([P, P]), identity[:])
            nc.scalar.copy(
                out=gates[:].rearrange("q (p m) -> q p m", p=P),
                in_=spread[:].rearrange("q m p -> q p m"),
            )

        def cast_weights(e, o, copy=nc.scalar.copy):
            copy(
                out=w_bf16[e, o][:].rearrange("p (c i) j -> p c j i", i=4),
                in_=w_raw[e, o].rearrange("p j (c i) -> p c j i", i=4),
            )

        def quantize_weights(e, o):
            nc.vector.quantize_mx(
                out=w_codes[e, o][:].bitcast(FP8X4),
                scales=w_scales[e, o][:],
                in_=w_bf16[e, o][:].rearrange("p n j -> p (n j)"),
            )

        def gather_words(o, first, count):
            nc.vector.tensor_copy(
                slot_words[o][:, first : first + count],
                token_words[o][:].bitcast(U32).indirect(entries(first, count)),
            )

        def multiply(e, o):
            slots = slice(e * C, (e + 1) * C)
            if o == 0:
                sums[e] = psum.tile([P, C], F32, name="sums%d" % e, tag="bank%d" % e)
            nc.tensor.matmul_mx(
                out=sums[e][:],
                lhsT=w_codes[e, o][:].bitcast(FP8X4),
                lhsT_scale=w_scales[e, o][:],
                rhs=slot_words[o][:, slots].bitcast(FP8X4),
                rhs_scale=slot_scales[4 * o : P, slots],
                start=(o == 0),
                stop=(o == PASSES - 1),
            )

        def activate(e, first, count, tag=""):
            values = keep.tile([P, count], F32, name="activated%d_%d" % (e, first), tag=tag, align_bytes=64)
            nc.scalar.activation(
                out=values[:], in_=sums[e][:, first : first + count], func=GELU, bias=bias[:, e : e + 1]
            )
            activated[e, first] = values

        def scatter(e, first, count):
            nc.vector.tensor_tensor(
                result[:].indirect(entries(e * C + first, count)),
                activated[e, first][:],
                gates[:, e * C + first : e * C + first + count],
                MULT,
            )

        load_tokens(0)
        nc.sync.dma_start(offsets[:], offs)
        load_scales()
        load_weights(0, 0, 2)
        load_tokens(1)
        load_gate()
        load_weights(0, 2, 1)
        load_tokens(2)
        load_weights(0, 3, 1)
        load_tokens(3)
        nc.sync.dma_start(out=bias[:], in_=b)
        load_weights(1, 0, 1, tag="second")
        load_weights(1, 1, 1)
        load_weights(1, 2, 1)
        load_weights(1, 3, 1, tag="last")
        gather_words(0, 0, S)
        nc.vector.tensor_copy(slot_scales[:], token_scales[:].indirect(offsets[:]))
        cast_weights(0, 0)
        cast_weights(0, 1)
        quantize_weights(0, 0)
        gather_words(1, 0, S)
        quantize_weights(0, 1)
        spread_gate()
        cast_weights(0, 2)
        cast_weights(0, 3)
        quantize_weights(0, 2)
        gather_words(2, 0, S)
        quantize_weights(0, 3)
        gather_words(3, 0, C)
        gather_words(3, C, C)
        for o in range(PASSES):
            multiply(0, o)
        cast_weights(1, 0)
        quantize_weights(1, 0)
        activate(0, 0, C // 2, tag="second")
        scatter(0, 0, C // 2)
        cast_weights(1, 1)
        cast_weights(1, 2, nc.vector.tensor_copy)
        quantize_weights(1, 1)
        quantize_weights(1, 2)
        cast_weights(1, 3)
        quantize_weights(1, 3)
        activate(0, C // 2, C // 2, tag="last")
        scatter(0, C // 2, C // 2)
        for o in range(PASSES):
            multiply(1, o)
        activate(1, 0, C)
        scatter(1, 0, C)
        nc.sync.dma_start(out=out, in_=result[:])
